import numpy as np, ml_dtypes
CORES = [24,26,29,31,48,50,53,55]
N = 8
import mx_ref
NC = 512
BF = ml_dtypes.bfloat16
def cut(t, i, w=512):
    return t[:, w * i:w * i + w]
def pk(c, s, i=0):
    return (np.ascontiguousarray(c[:, 512 * i:512 * i + 512]), mx_ref.live(s[:, 128 * i:128 * i + 128]))
def inputs(rng, e, E):
    def f(*shape):
        v = (rng.standard_normal(shape, dtype=np.float32) * np.exp2(rng.integers(-2, 3, shape[:-1] + (1,)))).astype(BF)
        return mx_ref.spread((v.astype(np.float32) * np.exp2(rng.integers(-E, E + 1, shape[:-2] + (1, 1))).astype(np.float32)).astype(BF), rng, e)
    def packed(k):
        c = np.zeros((N, 128, k * 512), np.uint8); s = np.zeros((N, 128, k * 128), np.uint8)
        for r in range(N):
            for i in range(k):
                a, b = mx_ref.quantize(f(128, 512)); c[r][:, 512 * i:512 * i + 512] = a; s[r][:, 128 * i:128 * i + 128] = mx_ref.plane(b, rng)
        return c, s
    d = {}
    d["wc"], d["ws"] = packed(N)
    d["x"] = f(N, 128, N * 4 * NC)
    return d
def setup_inputs(rng):
    return inputs(rng, 0, 0)
def setup_inputs_blocks(rng):
    return inputs(rng, 2, 0)
def setup_inputs_wide(rng):
    return inputs(rng, 0, 8)
def reference(wc, ws, x):
    y = np.zeros((N, 128, NC), np.float32)
    for r in range(N):
        for j in range(N):
            p = mx_ref.matmul(pk(wc[j], ws[j], r), mx_ref.quantize(cut(x[r], j, 4 * NC)))
            y[r] = p if j == 0 else y[r] + p
    return {"y": y}

@@ -1,0 +1,191 @@
+from concourse.bass import DstId, RemoteDMATransfer
+from concourse.mybir import dt, ActivationFunctionType
+
+NR = 8
+WT = 128
+XT = 512
+NB = 4
+BW = XT // NB
+SIM = 64
+FIRST = 1
+
+SCRATCH = {
+    "wq": ("sbuf", [128, NR * WT], "float8_e4m3fn_x4"),
+    "wp": ("sbuf", [128, NR * WT], "uint8"),
+    "rq": ("sbuf", [128, NR * WT], "float8_e4m3fn_x4"),
+    "rp": ("sbuf", [128, NR * WT], "uint8"),
+    "hq": ("sbuf", [128, 2 * NR * WT], "float8_e4m3fn_x4"),
+    "hp": ("sbuf", [128, 2 * NR * WT], "uint8"),
+    "xb": ("sbuf", [128, NR * 4 * XT], "bfloat16"),
+    "xq": ("sbuf", [128, NR * XT], "float8_e4m3fn_x4"),
+    "xs": ("sbuf", [128, NR * XT], "uint8"),
+    "ps": ("psum", [128, NB * 512], "float32"),
+    "yb": ("sbuf", [128, XT], "float32"),
+}
+SEMAPHORES = (["ls", "lc", "go", "sent", "st", "hs0", "hs1", "hc0", "hc1"]
+              + ["w%d" % j for j in range(NR)] + ["xl%d" % i for i in range(NR)]
+              + ["q%d" % i for i in range(NR + NB)] + ["mm%d" % b for b in range(NB)] + ["cp%d" % b for b in range(NB)])
+
+
+def _split(mask, k):
+    e = [i for i in range(mask.bit_length()) if (mask >> i) & 1]
+    per = 1
+    while per * 2 * k <= len(e):
+        per *= 2
+    return [sum(1 << b for b in e[i * per:(i + 1) * per]) for i in range(k)], per
+
+
+def _count(mask):
+    return sum((mask >> i) & 1 for i in range(mask.bit_length()))
+
+
+def _plan(T, topo):
+    cores = list(T.cores)
+    chip = [topo.chip(c) for c in cores]
+    calls, total, jobs, late = {}, {}, {}, {}
+
+    def free(ch, die, far_core, able):
+        for c in range(SIM):
+            if c not in cores and topo.chip(c) == ch and topo.die(c) == die and topo.may_write(c, far_core) == able:
+                return c
+
+    def add(core, wait, kind, trs):
+        calls.setdefault(core, []).append((wait, kind, trs))
+        for t in trs:
+            key = (t["to"], t["sem"])
+            total[key] = total.get(key, 0) + _count(t["mask"])
+
+    for j, c in enumerate(cores):
+        near = [i for i in range(NR) if chip[i] == chip[j]]
+        far = [i for i in range(NR) if chip[i] != chip[j]]
+        fc, nc = cores[far[0]], [cores[i] for i in near if i != j][0]
+        out = topo.mask(c, fc)
+        late[j] = not topo.may_write(c, fc)
+        if late[j]:
+            parts = [(0, NR, free(chip[j], topo.die(c), fc, True), 0, topo.mask(c, nc))]
+        else:
+            parts = [(far[0], far[-1] + 1, free(chip[far[0]], topo.die(c), c, False), 1, out),
+                     (near[0], near[-1] + 1, free(chip[j], topo.die(c), fc, False), 0, topo.mask(c, nc) & ~out)]
+        for kind in "sc":
+            add(c, "l" + kind, kind,
+                [dict(src="w", a=WT * lo, to=h, dst="h", b=slot * NR * WT + WT * lo, n=WT * (hi - lo), mask=m,
+                      sem="h%s%d" % (kind, slot)) for lo, hi, h, slot, m in parts])
+        for lo, hi, h, slot, m in parts:
+            jobs.setdefault(h, []).append((slot, j, lo, hi))
+
+    for h, js in jobs.items():
+        for kind in "sc":
+            for slot, j, lo, hi in sorted(js):
+                away = [d for d in range(lo, hi) if d != j and topo.chip(cores[d]) != topo.chip(h)]
+                home = [d for d in range(lo, hi) if d != j and topo.chip(cores[d]) == topo.chip(h)]
+                left = topo.mask(h, cores[home[0]])
+                pairs = []
+                if away:
+                    out = topo.mask(h, cores[away[0]])
+                    left &= ~out
+                    pairs += list(zip(away, _split(out, len(away))[0]))
+                pairs += list(zip(home, _split(left, len(home))[0]))
+                add(h, "h%s%d" % (kind, slot), kind,
+                    [dict(src="h", a=slot * NR * WT + WT * d, to=cores[d], dst="r", b=WT * j, n=WT, mask=m,
+                          sem="w%d" % j) for d, m in pairs])
+    return calls, total, late
+
+
+def _runs(tiles):
+    out = []
+    for t in sorted(tiles):
+        if out and out[-1][-1] + 1 == t:
+            out[-1].append(t)
+        else:
+            out.append([t])
+    return out
+
+
+def _remote(g, core, T, topo, calls, total):
+    sent = 0
+    for wait, kind, trs in calls.get(core, []):
+        g.wait_ge(T.sem[wait], total.get((core, wait), 16))
+        lst = []
+        for t in trs:
+            rid, pid, _se = topo.addr(t["to"])
+            if kind == "c":
+                s = T[t["src"] + "q"][:, t["a"]:t["a"] + t["n"]].bitcast(dt.uint8)
+                d = T[t["dst"] + "q"][:, t["b"]:t["b"] + t["n"]].bitcast(dt.uint8)
+            else:
+                s = T[t["src"] + "p"][:, t["a"]:t["a"] + t["n"]]
+                d = T[t["dst"] + "p"][:, t["b"]:t["b"] + t["n"]]
+            lst.append(RemoteDMATransfer(dst_ids=[DstId(rid=rid, pnc=pid)], dma_engine_mask=t["mask"],
+                                         remote_sem=T.sem[t["sem"]], src=s, dst=d))
+            sent += _count(t["mask"])
+        g.remote_dma_fused(lst, local_sem=T.sem.sent)
+    return sent
+
+
+def rank_program(g, core, T, topo):
+    calls, total, late = _plan(T, topo)
+    r = T.rank_of(core)
+    if r is None:
+        if core in calls:
+            g.wait_ge(T.sem.sent, _remote(g, core, T, topo, calls, total))
+        return
+
+    cores = list(T.cores)
+    near = [i for i in range(NR) if topo.chip(cores[i]) == topo.chip(core)]
+    far = [i for i in range(NR) if topo.chip(cores[i]) != topo.chip(core)]
+    far_order = [j for j in far if not late[j]] + [j for j in far if late[j]]
+    order = [r] + [j for j in near if j != r] + far_order
+    last = order[-1]
+    loads = [near[:FIRST]] + _runs(near[FIRST:]) + _runs([j for j in far if j != last]) + [[last]]
+
+    g.scalar.dma_start(T.wp[:], T.ws[:]).then_inc(T.sem.ls, 16)
+    g.sync.dma_start(T.wq[:].bitcast(dt.uint8), T.wc[:]).then_inc(T.sem.lc, 16)
+
+    for i, run in enumerate(loads):
+        if i == 1:
+            g.sync.wait_ge(T.sem.go, 1)
+        a, b = 4 * XT * run[0], 4 * XT * (run[-1] + 1)
+        g.sync.dma_start(T.xb[:, a:b], T.x[:, a:b]).then_inc(T.sem["xl%d" % i], 16)
+
+    sent = _remote(g, core, T, topo, calls, total)
+    g.sem_inc(T.sem.go, 1)
+    g.wait_ge(T.sem.sent, sent)
+
+    qsem, nq = {}, 0
+    for i, run in enumerate(loads):
+        g.vector.wait_ge(T.sem["xl%d" % i], 16)
+        for t in run:
+            step = BW if t == last else XT
+            for c0 in range(0, XT, step):
+                a = XT * t + c0
+                g.vector.quantize_mx(T.xq[:, a:a + step], T.xs[:, a:a + step],
+                                     T.xb[:, 4 * a:4 * (a + step)]).then_inc(T.sem["q%d" % nq], 1)
+                for b in range(c0 // BW, (c0 + step) // BW):
+                    qsem[(t, b)] = "q%d" % nq
+                nq += 1
+
+    for k, j in enumerate(order):
+        if j == r:
+            g.tensor.wait_ge(T.sem.ls, 16)
+            g.tensor.wait_ge(T.sem.lc, 16)
+            wq, wp, c0 = T.wq, T.wp, WT * r
+        else:
+            g.tensor.wait_ge(T.sem["w%d" % j], total[(core, "w%d" % j)])
+            wq, wp, c0 = T.rq, T.rp, WT * j
+        seen = None
+        for b in range(NB):
+            if qsem[(j, b)] != seen:
+                seen = qsem[(j, b)]
+                g.tensor.wait_ge(T.sem[seen], 1)
+            a = XT * j + BW * b
+            mm = g.tensor.matmul_mx(T.ps[:, 512 * b:512 * b + BW], wq[:, c0:c0 + WT], wp[:, c0:c0 + WT],
+                                    T.xq[:, a:a + BW], T.xs[:, a:a + BW], k == 0, k == NR - 1)
+            if k == NR - 1:
+                mm.then_inc(T.sem["mm%d" % b], 1)
+
+    for b in range(NB):
+        g.scalar.wait_ge(T.sem["mm%d" % b], 1)
+        g.scalar.activation(T.yb[:, BW * b:BW * (b + 1)], T.ps[:, 512 * b:512 * b + BW],
+                            ActivationFunctionType.Copy).then_inc(T.sem["cp%d" % b], 1)
+        g.sync.wait_ge(T.sem["cp%d" % b], 1)
+        g.sync.dma_start(T.y[:, BW * b:BW * (b + 1)], T.yb[:, BW * b:BW * (b + 1)]).then_inc(T.sem.st, 16)
+    g.sync.wait_ge(T.sem.st, 16 * NB)

@@ -7,7 +7,7 @@ XT = 512
 NB = 4
 BW = XT // NB
 SIM = 64
-FIRST = 1
+FIRST = 2
 
 SCRATCH = {
     "wq": ("sbuf", [128, NR * WT], "float8_e4m3fn_x4"),
@@ -22,8 +22,8 @@ SCRATCH = {
     "ps": ("psum", [128, NB * 512], "float32"),
     "yb": ("sbuf", [128, XT], "float32"),
 }
-SEMAPHORES = (["ls", "lc", "go", "sent", "st", "hs0", "hs1", "hc0", "hc1"]
-              + ["w%d" % j for j in range(NR)] + ["xl%d" % i for i in range(NR)]
+SEMAPHORES = (["ls", "lc", "go", "sent", "st", "st2", "hs0", "hs1", "hc0", "hc1"]
+              + ["w%d" % j for j in range(NR)] + ["xl%d" % i for i in range(NR + 1)]
               + ["q%d" % i for i in range(NR + NB)] + ["mm%d" % b for b in range(NB)] + ["cp%d" % b for b in range(NB)])
 
 
@@ -32,7 +32,7 @@ def _split(mask, k):
     per = 1
     while per * 2 * k <= len(e):
         per *= 2
-    return [sum(1 << b for b in e[i * per:(i + 1) * per]) for i in range(k)], per
+    return [sum(1 << b for b in e[i * per:(i + 1) * per]) for i in range(k)]
 
 
 def _count(mask):
@@ -45,9 +45,8 @@ def _plan(T, topo):
     calls, total, jobs, late = {}, {}, {}, {}
 
     def free(ch, die, far_core, able):
-        for c in range(SIM):
-            if c not in cores and topo.chip(c) == ch and topo.die(c) == die and topo.may_write(c, far_core) == able:
-                return c
+        return [c for c in range(SIM) if c not in cores and topo.chip(c) == ch and topo.die(c) == die
+                and topo.may_write(c, far_core) == able][0]
 
     def add(core, wait, kind, trs):
         calls.setdefault(core, []).append((wait, kind, trs))
@@ -55,6 +54,7 @@ def _plan(T, topo):
             key = (t["to"], t["sem"])
             total[key] = total.get(key, 0) + _count(t["mask"])
 
+    chips = sorted({topo.chip(c) for c in range(SIM)})
     for j, c in enumerate(cores):
         near = [i for i in range(NR) if chip[i] == chip[j]]
         far = [i for i in range(NR) if chip[i] != chip[j]]
@@ -62,43 +62,29 @@ def _plan(T, topo):
         out = topo.mask(c, fc)
         late[j] = not topo.may_write(c, fc)
         if late[j]:
-            parts = [(0, NR, free(chip[j], topo.die(c), fc, True), 0, topo.mask(c, nc))]
+            m = [a for a in chips if topo.mates(a, chip[far[0]]) and topo.same_plane(a, chip[j])][0]
+            fh = free(m, topo.die(c), fc, True)
         else:
-            parts = [(far[0], far[-1] + 1, free(chip[far[0]], topo.die(c), c, False), 1, out),
-                     (near[0], near[-1] + 1, free(chip[j], topo.die(c), fc, False), 0, topo.mask(c, nc) & ~out)]
+            fh = free(chip[far[0]], topo.die(c), c, False)
+        parts = [(far[0], far[-1] + 1, fh, 0, out),
+                 (near[0], near[-1] + 1, free(chip[j], topo.die(c), fc, True), 0 if late[j] else 1,
+                  topo.mask(c, nc) & ~out)]
         for kind in "sc":
             add(c, "l" + kind, kind,
-                [dict(src="w", a=WT * lo, to=h, dst="h", b=slot * NR * WT + WT * lo, n=WT * (hi - lo), mask=m,
-                      sem="h%s%d" % (kind, slot)) for lo, hi, h, slot, m in parts])
-        for lo, hi, h, slot, m in parts:
+                [dict(src="w", a=WT * lo, to=h, dst="h", b=slot * NR * WT + WT * lo, n=WT * (hi - lo), mask=m_,
+                      sem="h%s%d" % (kind, slot)) for lo, hi, h, slot, m_ in parts])
+        for lo, hi, h, slot, m_ in parts:
             jobs.setdefault(h, []).append((slot, j, lo, hi))
 
     for h, js in jobs.items():
         for kind in "sc":
             for slot, j, lo, hi in sorted(js):
-                away = [d for d in range(lo, hi) if d != j and topo.chip(cores[d]) != topo.chip(h)]
-                home = [d for d in range(lo, hi) if d != j and topo.chip(cores[d]) == topo.chip(h)]
-                left = topo.mask(h, cores[home[0]])
-                pairs = []
-                if away:
-                    out = topo.mask(h, cores[away[0]])
-                    left &= ~out
-                    pairs += list(zip(away, _split(out, len(away))[0]))
-                pairs += list(zip(home, _split(left, len(home))[0]))
+                dests = [d for d in range(lo, hi) if d != j]
+                masks = _split(topo.mask(h, cores[dests[0]]), len(dests))
                 add(h, "h%s%d" % (kind, slot), kind,
                     [dict(src="h", a=slot * NR * WT + WT * d, to=cores[d], dst="r", b=WT * j, n=WT, mask=m,
-                          sem="w%d" % j) for d, m in pairs])
+                          sem="w%d" % j) for d, m in zip(dests, masks)])
     return calls, total, late
-
-
-def _runs(tiles):
-    out = []
-    for t in sorted(tiles):
-        if out and out[-1][-1] + 1 == t:
-            out[-1].append(t)
-        else:
-            out.append([t])
-    return out
 
 
 def _remote(g, core, T, topo, calls, total):
@@ -135,33 +121,32 @@ def rank_program(g, core, T, topo):
     far_order = [j for j in far if not late[j]] + [j for j in far if late[j]]
     order = [r] + [j for j in near if j != r] + far_order
     last = order[-1]
-    loads = [near[:FIRST]] + _runs(near[FIRST:]) + _runs([j for j in far if j != last]) + [[last]]
+    loads = ([(XT * near[0], XT * (near[FIRST - 1] + 1))] + [(XT * t, XT * (t + 1)) for t in near[FIRST:]]
+             + [(XT * t, XT * (t + 1)) for t in far_order[:-1]]
+             + [(XT * last, XT * last + XT // 2), (XT * last + XT // 2, XT * (last + 1))])
 
     g.scalar.dma_start(T.wp[:], T.ws[:]).then_inc(T.sem.ls, 16)
     g.sync.dma_start(T.wq[:].bitcast(dt.uint8), T.wc[:]).then_inc(T.sem.lc, 16)
 
-    for i, run in enumerate(loads):
+    for i, (a, b) in enumerate(loads):
         if i == 1:
             g.sync.wait_ge(T.sem.go, 1)
-        a, b = 4 * XT * run[0], 4 * XT * (run[-1] + 1)
-        g.sync.dma_start(T.xb[:, a:b], T.x[:, a:b]).then_inc(T.sem["xl%d" % i], 16)
+        g.sync.dma_start(T.xb[:, 4 * a:4 * b], T.x[:, 4 * a:4 * b]).then_inc(T.sem["xl%d" % i], 16)
 
     sent = _remote(g, core, T, topo, calls, total)
     g.sem_inc(T.sem.go, 1)
     g.wait_ge(T.sem.sent, sent)
 
     qsem, nq = {}, 0
-    for i, run in enumerate(loads):
+    for i, (lo, hi) in enumerate(loads):
         g.vector.wait_ge(T.sem["xl%d" % i], 16)
-        for t in run:
-            step = BW if t == last else XT
-            for c0 in range(0, XT, step):
-                a = XT * t + c0
-                g.vector.quantize_mx(T.xq[:, a:a + step], T.xs[:, a:a + step],
-                                     T.xb[:, 4 * a:4 * (a + step)]).then_inc(T.sem["q%d" % nq], 1)
-                for b in range(c0 // BW, (c0 + step) // BW):
-                    qsem[(t, b)] = "q%d" % nq
-                nq += 1
+        step = BW if lo // XT == last else XT
+        for a in range(lo, hi, step):
+            g.vector.quantize_mx(T.xq[:, a:a + step], T.xs[:, a:a + step],
+                                 T.xb[:, 4 * a:4 * (a + step)]).then_inc(T.sem["q%d" % nq], 1)
+            for c in range(a, a + step, BW):
+                qsem[(c // XT, (c % XT) // BW)] = "q%d" % nq
+            nq += 1
 
     for k, j in enumerate(order):
         if j == r:
@@ -186,6 +171,8 @@ def rank_program(g, core, T, topo):
         g.scalar.wait_ge(T.sem["mm%d" % b], 1)
         g.scalar.activation(T.yb[:, BW * b:BW * (b + 1)], T.ps[:, 512 * b:512 * b + BW],
                             ActivationFunctionType.Copy).then_inc(T.sem["cp%d" % b], 1)
-        g.sync.wait_ge(T.sem["cp%d" % b], 1)
-        g.sync.dma_start(T.y[:, BW * b:BW * (b + 1)], T.yb[:, BW * b:BW * (b + 1)]).then_inc(T.sem.st, 16)
-    g.sync.wait_ge(T.sem.st, 16 * NB)
+        q, sem = (g.sync, T.sem.st) if b < NB - 1 else (g.scalar, T.sem.st2)
+        q.wait_ge(T.sem["cp%d" % b], 1)
+        q.dma_start(T.y[:, BW * b:BW * (b + 1)], T.yb[:, BW * b:BW * (b + 1)]).then_inc(sem, 16)
+    g.sync.wait_ge(T.sem.st, 16 * (NB - 1))
+    g.scalar.wait_ge(T.sem.st2, 16)

from concourse.bass import DstId, RemoteDMATransfer
from concourse.mybir import dt, ActivationFunctionType

NR = 8
WT = 128
XT = 512
NB = 4
BW = XT // NB
SIM = 64
FIRST = 2

SCRATCH = {
    "wq": ("sbuf", [128, NR * WT], "float8_e4m3fn_x4"),
    "wp": ("sbuf", [128, NR * WT], "uint8"),
    "rq": ("sbuf", [128, NR * WT], "float8_e4m3fn_x4"),
    "rp": ("sbuf", [128, NR * WT], "uint8"),
    "hq": ("sbuf", [128, 2 * NR * WT], "float8_e4m3fn_x4"),
    "hp": ("sbuf", [128, 2 * NR * WT], "uint8"),
    "xb": ("sbuf", [128, NR * 4 * XT], "bfloat16"),
    "xq": ("sbuf", [128, NR * XT], "float8_e4m3fn_x4"),
    "xs": ("sbuf", [128, NR * XT], "uint8"),
    "ps": ("psum", [128, NB * 512], "float32"),
    "yb": ("sbuf", [128, XT], "float32"),
}
SEMAPHORES = (["ls", "lc", "go", "sent", "st", "st2", "hs0", "hs1", "hc0", "hc1"]
              + ["w%d" % j for j in range(NR)] + ["xl%d" % i for i in range(NR + 1)]
              + ["q%d" % i for i in range(NR + NB)] + ["mm%d" % b for b in range(NB)] + ["cp%d" % b for b in range(NB)])


def _split(mask, k):
    e = [i for i in range(mask.bit_length()) if (mask >> i) & 1]
    per = 1
    while per * 2 * k <= len(e):
        per *= 2
    return [sum(1 << b for b in e[i * per:(i + 1) * per]) for i in range(k)]


def _count(mask):
    return sum((mask >> i) & 1 for i in range(mask.bit_length()))


def _plan(T, topo):
    cores = list(T.cores)
    chip = [topo.chip(c) for c in cores]
    calls, total, jobs, late = {}, {}, {}, {}

    def free(ch, die, far_core, able):
        return [c for c in range(SIM) if c not in cores and topo.chip(c) == ch and topo.die(c) == die
                and topo.may_write(c, far_core) == able][0]

    def add(core, wait, kind, trs):
        calls.setdefault(core, []).append((wait, kind, trs))
        for t in trs:
            key = (t["to"], t["sem"])
            total[key] = total.get(key, 0) + _count(t["mask"])

    chips = sorted({topo.chip(c) for c in range(SIM)})
    for j, c in enumerate(cores):
        near = [i for i in range(NR) if chip[i] == chip[j]]
        far = [i for i in range(NR) if chip[i] != chip[j]]
        fc, nc = cores[far[0]], [cores[i] for i in near if i != j][0]
        out = topo.mask(c, fc)
        late[j] = not topo.may_write(c, fc)
        if late[j]:
            m = [a for a in chips if topo.mates(a, chip[far[0]]) and topo.same_plane(a, chip[j])][0]
            fh = free(m, topo.die(c), fc, True)
        else:
            fh = free(chip[far[0]], topo.die(c), c, False)
        parts = [(far[0], far[-1] + 1, fh, 0, out),
                 (near[0], near[-1] + 1, free(chip[j], topo.die(c), fc, True), 0 if late[j] else 1,
                  topo.mask(c, nc) & ~out)]
        for kind in "sc":
            add(c, "l" + kind, kind,
                [dict(src="w", a=WT * lo, to=h, dst="h", b=slot * NR * WT + WT * lo, n=WT * (hi - lo), mask=m_,
                      sem="h%s%d" % (kind, slot)) for lo, hi, h, slot, m_ in parts])
        for lo, hi, h, slot, m_ in parts:
            jobs.setdefault(h, []).append((slot, j, lo, hi))

    for h, js in jobs.items():
        for kind in "sc":
            for slot, j, lo, hi in sorted(js):
                dests = [d for d in range(lo, hi) if d != j]
                masks = _split(topo.mask(h, cores[dests[0]]), len(dests))
                add(h, "h%s%d" % (kind, slot), kind,
                    [dict(src="h", a=slot * NR * WT + WT * d, to=cores[d], dst="r", b=WT * j, n=WT, mask=m,
                          sem="w%d" % j) for d, m in zip(dests, masks)])
    return calls, total, late


def _remote(g, core, T, topo, calls, total):
    sent = 0
    for wait, kind, trs in calls.get(core, []):
        g.wait_ge(T.sem[wait], total.get((core, wait), 16))
        lst = []
        for t in trs:
            rid, pid, _se = topo.addr(t["to"])
            if kind == "c":
                s = T[t["src"] + "q"][:, t["a"]:t["a"] + t["n"]].bitcast(dt.uint8)
                d = T[t["dst"] + "q"][:, t["b"]:t["b"] + t["n"]].bitcast(dt.uint8)
            else:
                s = T[t["src"] + "p"][:, t["a"]:t["a"] + t["n"]]
                d = T[t["dst"] + "p"][:, t["b"]:t["b"] + t["n"]]
            lst.append(RemoteDMATransfer(dst_ids=[DstId(rid=rid, pnc=pid)], dma_engine_mask=t["mask"],
                                         remote_sem=T.sem[t["sem"]], src=s, dst=d))
            sent += _count(t["mask"])
        g.remote_dma_fused(lst, local_sem=T.sem.sent)
    return sent


def rank_program(g, core, T, topo):
    calls, total, late = _plan(T, topo)
    r = T.rank_of(core)
    if r is None:
        if core in calls:
            g.wait_ge(T.sem.sent, _remote(g, core, T, topo, calls, total))
        return

    cores = list(T.cores)
    near = [i for i in range(NR) if topo.chip(cores[i]) == topo.chip(core)]
    far = [i for i in range(NR) if topo.chip(cores[i]) != topo.chip(core)]
    far_order = [j for j in far if not late[j]] + [j for j in far if late[j]]
    order = [r] + [j for j in near if j != r] + far_order
    last = order[-1]
    loads = ([(XT * near[0], XT * (near[FIRST - 1] + 1))] + [(XT * t, XT * (t + 1)) for t in near[FIRST:]]
             + [(XT * t, XT * (t + 1)) for t in far_order[:-1]]
             + [(XT * last, XT * last + XT // 2), (XT * last + XT // 2, XT * (last + 1))])

    g.scalar.dma_start(T.wp[:], T.ws[:]).then_inc(T.sem.ls, 16)
    g.sync.dma_start(T.wq[:].bitcast(dt.uint8), T.wc[:]).then_inc(T.sem.lc, 16)

    for i, (a, b) in enumerate(loads):
        if i == 1:
            g.sync.wait_ge(T.sem.go, 1)
        g.sync.dma_start(T.xb[:, 4 * a:4 * b], T.x[:, 4 * a:4 * b]).then_inc(T.sem["xl%d" % i], 16)

    sent = _remote(g, core, T, topo, calls, total)
    g.sem_inc(T.sem.go, 1)
    g.wait_ge(T.sem.sent, sent)

    qsem, nq = {}, 0
    for i, (lo, hi) in enumerate(loads):
        g.vector.wait_ge(T.sem["xl%d" % i], 16)
        step = BW if lo // XT == last else XT
        for a in range(lo, hi, step):
            g.vector.quantize_mx(T.xq[:, a:a + step], T.xs[:, a:a + step],
                                 T.xb[:, 4 * a:4 * (a + step)]).then_inc(T.sem["q%d" % nq], 1)
            for c in range(a, a + step, BW):
                qsem[(c // XT, (c % XT) // BW)] = "q%d" % nq
            nq += 1

    for k, j in enumerate(order):
        if j == r:
            g.tensor.wait_ge(T.sem.ls, 16)
            g.tensor.wait_ge(T.sem.lc, 16)
            wq, wp, c0 = T.wq, T.wp, WT * r
        else:
            g.tensor.wait_ge(T.sem["w%d" % j], total[(core, "w%d" % j)])
            wq, wp, c0 = T.rq, T.rp, WT * j
        seen = None
        for b in range(NB):
            if qsem[(j, b)] != seen:
                seen = qsem[(j, b)]
                g.tensor.wait_ge(T.sem[seen], 1)
            a = XT * j + BW * b
            mm = g.tensor.matmul_mx(T.ps[:, 512 * b:512 * b + BW], wq[:, c0:c0 + WT], wp[:, c0:c0 + WT],
                                    T.xq[:, a:a + BW], T.xs[:, a:a + BW], k == 0, k == NR - 1)
            if k == NR - 1:
                mm.then_inc(T.sem["mm%d" % b], 1)

    for b in range(NB):
        g.scalar.wait_ge(T.sem["mm%d" % b], 1)
        g.scalar.activation(T.yb[:, BW * b:BW * (b + 1)], T.ps[:, 512 * b:512 * b + BW],
                            ActivationFunctionType.Copy).then_inc(T.sem["cp%d" % b], 1)
        q, sem = (g.sync, T.sem.st) if b < NB - 1 else (g.scalar, T.sem.st2)
        q.wait_ge(T.sem["cp%d" % b], 1)
        q.dma_start(T.y[:, BW * b:BW * (b + 1)], T.yb[:, BW * b:BW * (b + 1)]).then_inc(sem, 16)
    g.sync.wait_ge(T.sem.st, 16 * (NB - 1))
    g.scalar.wait_ge(T.sem.st2, 16)
